import numpy as np
import ml_dtypes


def mxq(x, axis, fmt="e4m3"):
    dtype, down = {"e4m3": (ml_dtypes.float8_e4m3fn, 7), "e5m2": (ml_dtypes.float8_e5m2, 14)}[fmt]
    v = np.moveaxis(np.asarray(x, np.float32).astype(ml_dtypes.bfloat16).astype(np.float64), axis, -1)
    blocks = v.reshape(v.shape[:-1] + (-1, 32))
    amax = np.abs(blocks).max(-1, keepdims=True)
    byte = np.maximum(np.where(amax > 0, np.frexp(amax)[1] - 1 + 127, 0) - down, 1)
    scale = np.exp2(byte - 127.0)
    codes = (blocks / scale).astype(np.float32).astype(dtype).astype(np.float64)
    return np.moveaxis((codes * scale).reshape(v.shape), -1, axis)


WIDE = False


def mx_kscale(k):
    if not WIDE:
        return np.ones(k)
    levels = np.array([10, -10, 5, -5, 0])
    if k % 512:
        return np.exp2(np.random.permutation(np.resize(levels, k // 32))).repeat(32)
    a = np.empty((k // 512, 16))
    for p in range(k // 512):
        a[p, :8] = np.random.permutation(np.resize(levels, 8))
        for g in range(8):
            far = levels[np.abs(levels - a[p, g]) >= 10]
            a[p, g + 8] = far[np.random.randint(len(far))]
    return np.exp2(a.ravel()).repeat(32)


def f64(x):
    return np.asarray(x).astype(np.float64)


def striped(idx):
    return np.tile(idx.reshape(-1, 16).T, (8, 1)).astype(np.uint16)


def unstriped(offs):
    return offs[:16].T.reshape(-1).astype(np.int64)


E2M1 = np.array([0.0, 0.5, 1.0, 1.5, 2.0, 3.0, 4.0, 6.0, -0.0, -0.5, -1.0, -1.5, -2.0, -3.0, -4.0, -6.0])


def pack_weight(w, fmt):
    k, n = w.shape
    w = f64(np.asarray(w, np.float32).astype(ml_dtypes.bfloat16)).reshape(k // 32, 32, n)
    amax = np.abs(w).max(1)
    if fmt == "e4m3":
        byte = np.frexp(amax)[1] - 1 + 127 - 7
    else:
        mant, ex = np.frexp(amax / 6.0)
        byte = np.where(mant > 0.5, ex, ex - 1) + 127
    byte = np.clip(np.where(amax > 0, byte, 1), 1, 254)
    scaled = (w * np.exp2(127.0 - byte)[:, None, :]).reshape(k, n).astype(np.float32)
    by_word = np.ascontiguousarray(scaled.reshape(k // 512, 128, 4, n).transpose(0, 1, 3, 2))
    if fmt == "e4m3":
        words = by_word.astype(ml_dtypes.float8_e4m3fn).view(np.uint8)
    else:
        c = by_word.astype(ml_dtypes.float4_e2m1fn).view(np.uint8) & 0xF
        words = (c[..., 0::2] | (c[..., 1::2] << 4)).reshape(k // 512, 128, 2 * n)
    return np.ascontiguousarray(words), np.ascontiguousarray(byte.astype(np.uint8).reshape(k // 512, 16, n))


def unpack_weight(words, scales, fmt):
    g, _, n = scales.shape
    words = np.ascontiguousarray(words).reshape(g, 128, n, -1)
    if fmt == "e4m3":
        vals = words.view(ml_dtypes.float8_e4m3fn).astype(np.float64)
    else:
        nib = np.empty((g, 128, n, 4), np.uint8)
        nib[..., 0::2] = words & 0xF
        nib[..., 1::2] = words >> 4
        vals = E2M1[nib]
    vals = vals * np.repeat(np.exp2(scales.astype(np.float64) - 127.0), 8, axis=1)[..., None]
    return vals.transpose(0, 1, 3, 2).reshape(g * 512, n)


def gelu(v):
    return 0.5 * v * (1.0 + np.tanh(np.sqrt(2.0 / np.pi) * (v + 0.044715 * v**3)))


K, H, T, S, P = 1024, 1024, 4096, 1024, 512


def setup_inputs():
    n = np.random.standard_normal
    s = mx_kscale(K)[:, None]
    u = mx_kscale(H)[:, None]
    tab_words, tab_scales = pack_weight(n((K, T)) * s, "e4m3")
    w1 = (n((K, H)) / np.sqrt(K) / s * u.T).astype(np.float32)
    w2_words, w2_scales = pack_weight(n((H, H)) / np.sqrt(H) / u, "e2m1")
    w3 = (0.5 * n((H, H)) / np.sqrt(H) / u).astype(np.float32)
    return {
        "tab_words": tab_words, "tab_scales": tab_scales,
        "offs": striped(np.random.permutation(T)[:S]),
        "pos1": striped(np.random.permutation(S)[:P]),
        "w1": w1,
        "density": (n((H, S)) * u).astype(np.float32),
        "gain": np.exp(0.3 * n(H)).astype(np.float32),
        "w2_words": w2_words, "w2_scales": w2_scales,
        "azim": np.random.uniform(-1.73, 1.73, (H, P)).astype(np.float32),
        "w3": w3,
        "skip": (0.5 * np.exp(0.3 * n(H)) / u[:, 0]).astype(np.float32),
        "wgo": np.exp(0.3 * n((128, P))).astype(np.float32),
    }


def reference(tab_words, tab_scales, offs, pos1, w1, density, gain, w2_words, w2_scales, azim, w3, skip, wgo):
    v = unpack_weight(tab_words, tab_scales, "e4m3")[:, unstriped(offs)]
    a = mxq(f64(w1), 0, "e4m3").T @ v
    h = f64(gain)[:, None] * np.maximum(a, f64(density))
    x = h[:, unstriped(pos1)]
    x1 = mxq(x, 0, "e4m3")
    x2 = mxq(f64(azim) * x, 0, "e4m3")
    e1 = unpack_weight(w2_words, w2_scales, "e2m1").T @ x1
    e2 = mxq(f64(w3), 0, "e4m3").T @ x2
    y = np.tanh(e1) + np.sin(e2)
    out = f64(skip)[:, None] * h
    out[:, unstriped(pos1)] = np.tile(f64(wgo), (H // 128, 1)) * y
    return out

@@ -1,0 +1,313 @@
+import math
+from contextlib import ExitStack
+
+import concourse.mybir as mybir
+
+K, H, T, S, M = 1024, 1024, 4096, 1024, 512
+FLOPS = 2 * K * H * S + 2 * 2 * H * H * M
+
+F32 = mybir.dt.float32
+BF16 = mybir.dt.bfloat16
+I32 = mybir.dt.int32
+U32 = mybir.dt.uint32
+U16 = mybir.dt.uint16
+U8 = mybir.dt.uint8
+E4M3 = mybir.dt.float8_e4m3fn_x4
+E2M1 = mybir.dt.float4_e2m1fn_x4
+ALU = mybir.AluOpType
+ACT = mybir.ActivationFunctionType
+
+P = 128
+PACK = 4
+PASS = P * PACK
+PASSES = 2
+BANK = 512
+ROUND_BIAS = 1.5 * 2.0**23
+
+
+def tile_list_soundtrack_slit_restorer_kernel(
+    tc, tab_words, tab_scales, offs, pos1, w1, density, gain, w2_words, w2_scales, azim, w3, skip, wgo, out
+):
+    nc = tc.nc
+    with ExitStack() as ctx:
+        keep = ctx.enter_context(tc.tile_pool(name="keep", bufs=1))
+        ring = ctx.enter_context(tc.tile_pool(name="ring", bufs=2))
+        psum = ctx.enter_context(tc.psum_pool(name="psum", bufs=1))
+
+        slit_list = keep.tile([P, S // 16], U16, name="slit_list")
+        error_list = keep.tile([P, M // 16], U16, name="error_list")
+        table_scales = keep.tile([P, T], U8, name="table_scales", align_bytes=64)
+        w2_scales_raw = keep.tile([P, PASSES, H], U8, name="w2_scales_raw", align_bytes=64)
+        w2_raw = keep.tile([P, PASSES, 2 * H], U8, name="w2_raw", align_bytes=64)
+        gain_sb = keep.tile([P, PASSES, PACK], F32, name="gain_sb")
+        skip_sb = keep.tile([P, PASSES, PACK], F32, name="skip_sb")
+
+        nc.vector.memset(w2_scales_raw[:].rearrange("p a c -> p (a c)").bitcast(I32), 0)
+        nc.vector.memset(table_scales[:].bitcast(I32), 0)
+
+        nc.sync.dma_start(slit_list[:], offs)
+        nc.sync.dma_start(out=w2_raw[:].bitcast(I32), in_=w2_words.rearrange("a p c -> p a c").bitcast(I32))
+        for q in range(4):
+            nc.scalar.dma_start(
+                out=w2_scales_raw[32 * q : 32 * q + 4, :, :].bitcast(I32),
+                in_=w2_scales[:, 4 * q : 4 * q + 4, :].rearrange("a r c -> r a c").bitcast(I32),
+            )
+        for q in range(4):
+            nc.scalar.dma_start(
+                out=table_scales[32 * q : 32 * q + 4 * PASSES, :].bitcast(I32),
+                in_=tab_scales[:, 4 * q : 4 * q + 4, :].bitcast(I32),
+            )
+        nc.scalar.dma_start(out=gain_sb[:], in_=gain.rearrange("(b p t) -> p b t", p=P, t=PACK))
+        nc.scalar.dma_start(out=skip_sb[:], in_=skip.rearrange("(b p t) -> p b t", p=P, t=PACK))
+
+        table = []
+        for a in range(PASSES):
+            words = keep.tile([P, T], I32, name=f"table{a}", align_bytes=64)
+            nc.sync.dma_start(out=words[:], in_=tab_words[a].rearrange("p t i -> p (t i)").bitcast(I32))
+            table.append(words)
+        nc.sync.dma_start(error_list[:], pos1)
+
+        w2_codes = keep.tile([P, PASSES, 2 * H], U8, name="w2_codes", align_bytes=64)
+        w2_planes = keep.tile([P, PASSES, H], U8, name="w2_planes", align_bytes=64)
+        nc.vector.tensor_copy(
+            out=w2_codes[:].rearrange("p a c -> p (a c)").bitcast(U16).rearrange("p (g t q) -> p g q t", t=PACK, q=P),
+            in_=w2_raw[:].rearrange("p a c -> p (a c)").bitcast(U16).rearrange("p (g q t) -> p g q t", t=PACK, q=P),
+        )
+        nc.vector.tensor_copy(
+            out=w2_planes[:].rearrange("p a (b t q) -> p (a b) q t", t=PACK, q=P),
+            in_=w2_scales_raw[:].rearrange("p a (b q t) -> p (a b) q t", t=PACK, q=P),
+        )
+
+        kept_scale = keep.tile([P, PASSES, PACK], F32, name="kept_scale")
+        nc.vector.tensor_tensor(out=kept_scale[:], in0=gain_sb[:], in1=skip_sb[:], op=ALU.mult)
+
+        v_scales = keep.tile([P, S], U8, name="v_scales", align_bytes=64)
+        nc.vector.tensor_copy(v_scales[:], table_scales[:].indirect(slit_list[:]))
+        v_codes = []
+        for a in range(PASSES):
+            picked = keep.tile([P, S], U32, name=f"v_codes{a}", align_bytes=64)
+            nc.vector.tensor_copy(picked[:], table[a][:].bitcast(U32).indirect(slit_list[:]))
+            v_codes.append(picked)
+
+        def load_weight(w, a, b):
+            raw = ring.tile([P, PACK, PASS], F32, name="w_raw", bufs=3)
+            rows = w[PASS * a : PASS * (a + 1), PASS * b : PASS * (b + 1)]
+            nc.sync.dma_start(out=raw[:], in_=rows.rearrange("(p j) c -> p j c", j=PACK))
+            return raw
+
+        def round_weight(raw, copy, t0, t1):
+            rounded = ring.tile([P, t1 - t0, P, PACK], BF16, name="w_rounded", bufs=3, align_bytes=64)
+            copy(
+                out=rounded[:].rearrange("p t q j -> p q j t"),
+                in_=raw[:].rearrange("p j (q t) -> p q j t", t=PACK)[:, :, :, t0:t1],
+            )
+            return rounded
+
+        def new_operand(name, bufs):
+            codes = ring.tile([P, PASS], U32, name=name + "_codes", bufs=bufs, align_bytes=64)
+            plane = ring.tile([P, PASS], U8, name=name + "_plane", bufs=bufs, align_bytes=64)
+            return codes, plane
+
+        def quantize(operand, rounded, c0, c1):
+            codes, plane = operand
+            nc.vector.quantize_mx(out=codes[:, c0:c1].bitcast(E4M3), scales=plane[:, c0:c1], in_=rounded)
+
+        def quantize_weight(rounded):
+            operand = new_operand("w", 4)
+            quantize(operand, rounded[:].rearrange("p t q j -> p (t q j)"), 0, PASS)
+            return operand
+
+        pages = {}
+
+        def load_density(b, t):
+            page = keep.tile([P, S], F32, name=f"page{b}{t}")
+            nc.sync.dma_start(out=page[:], in_=density.rearrange("(b p t) j -> b t p j", p=P, t=PACK)[b, t])
+            pages[b, t] = page
+
+        def load_azim(b):
+            rows = ring.tile([P, PACK, M], F32, name="azim_rows", bufs=1)
+            nc.sync.dma_start(out=rows[:], in_=azim[PASS * b : PASS * (b + 1), :].rearrange("(p t) m -> p t m", t=PACK))
+            return rows
+
+        def features(w1_ops, b, t):
+            page = pages[b, t]
+            cols = slice(P * t, P * (t + 1))
+            for j0 in range(0, S, BANK):
+                slits = slice(j0, j0 + BANK)
+                acc = psum.tile([P, BANK], F32, name="feature_acc", bufs=4)
+                for a in range(PASSES):
+                    codes, plane = w1_ops[a]
+                    nc.tensor.matmul_mx(
+                        out=acc[:],
+                        lhsT=codes[:, cols].bitcast(E4M3),
+                        lhsT_scale=plane[:, cols],
+                        rhs=v_codes[a][:, slits].bitcast(E4M3),
+                        rhs_scale=v_scales[4 * a : P, slits],
+                        start=(a == 0),
+                        stop=(a == PASSES - 1),
+                    )
+                nc.vector.tensor_tensor(out=page[:, slits], in0=acc[:], in1=page[:, slits], op=ALU.max)
+
+        def pick(picked, b, t):
+            page = pages[b, t]
+            nc.vector.tensor_copy(picked[:, t, :], page[:].indirect(error_list[:]))
+            nc.scalar.activation(
+                out=picked[:, t, :], in_=picked[:, t, :], func=ACT.Copy, scale=gain_sb[:, b, t : t + 1]
+            )
+
+        def scale_page(b, t):
+            page = pages[b, t]
+            nc.scalar.activation(out=page[:], in_=page[:], func=ACT.Copy, scale=kept_scale[:, b, t : t + 1])
+
+        def make_x(picked, azim_rows):
+            x1 = ring.tile([P, M * PACK], BF16, name="x1_rounded", bufs=1, align_bytes=64)
+            x2 = ring.tile([P, M * PACK], BF16, name="x2_rounded", bufs=1, align_bytes=64)
+            src = picked[:].rearrange("p t (c i) -> p c t i", i=4)
+            nc.scalar.copy(out=x1[:].rearrange("p (c i t) -> p c t i", i=4, t=PACK), in_=src)
+            nc.vector.tensor_tensor(
+                out=x2[:].rearrange("p (c i t) -> p c t i", i=4, t=PACK),
+                in0=src,
+                in1=azim_rows[:].rearrange("p t (c i) -> p c t i", i=4),
+                op=ALU.mult,
+            )
+            return x1, x2
+
+        def quantize_x(name, rounded):
+            operand = new_operand(name, 2)
+            quantize(operand, rounded[:], 0, M)
+            return operand
+
+        raw00 = load_weight(w1, 0, 0)
+        raw10 = load_weight(w1, 1, 0)
+        load_density(0, 0)
+        load_density(0, 1)
+        raw01 = load_weight(w1, 0, 1)
+        load_density(0, 2)
+        w1_b0 = [quantize_weight(round_weight(raw00, nc.scalar.copy, 0, PACK))]
+        last = new_operand("w", 4)
+        low = round_weight(raw10, nc.vector.tensor_copy, 0, 2)
+        high = round_weight(raw10, nc.scalar.copy, 2, 4)
+        quantize(last, low[:].rearrange("p t q j -> p (t q j)"), 0, 2 * P)
+        quantize(last, high[:].rearrange("p t q j -> p (t q j)"), 2 * P, 4 * P)
+        w1_b0.append(last)
+        raw11 = load_weight(w1, 1, 1)
+        load_density(0, 3)
+        azim0 = load_azim(0)
+        for t in range(PACK):
+            load_density(1, t)
+
+        picked0 = ring.tile([P, PACK, M], F32, name="picked")
+        features(w1_b0, 0, 0)
+        features(w1_b0, 0, 1)
+        pick(picked0, 0, 0)
+        rounded01 = round_weight(raw01, nc.scalar.copy, 0, PACK)
+        features(w1_b0, 0, 2)
+        pick(picked0, 0, 1)
+        rounded11 = round_weight(raw11, nc.scalar.copy, 0, PACK)
+        features(w1_b0, 0, 3)
+        w1_b1 = [quantize_weight(rounded01)]
+        pick(picked0, 0, 2)
+        w1_b1.append(quantize_weight(rounded11))
+        pick(picked0, 0, 3)
+        w3raw00 = load_weight(w3, 0, 0)
+        w3raw10 = load_weight(w3, 1, 0)
+
+        picked1 = ring.tile([P, PACK, M], F32, name="picked")
+        features(w1_b1, 1, 0)
+        x1a, x2a = make_x(picked0, azim0)
+        azim1 = load_azim(1)
+        wgo_rows = keep.tile([P, PACK, M], F32, name="wgo_rows")
+        for q in range(4):
+            nc.sync.dma_start(out=wgo_rows[32 * q : 32 * (q + 1)], in_=wgo.rearrange("(p t) m -> p t m", t=PACK))
+        features(w1_b1, 1, 1)
+        pick(picked1, 1, 0)
+        x2_ops = [quantize_x("x2", x2a)]
+        x1_ops = [quantize_x("x1", x1a)]
+        scale_page(0, 0)
+        scale_page(0, 1)
+        features(w1_b1, 1, 2)
+        pick(picked1, 1, 1)
+        rounded_a = round_weight(w3raw00, nc.scalar.copy, 0, PACK)
+        features(w1_b1, 1, 3)
+        pick(picked1, 1, 2)
+        rounded_b = round_weight(w3raw10, nc.scalar.copy, 0, PACK)
+        w3_b0 = [quantize_weight(rounded_a)]
+        pick(picked1, 1, 3)
+        w3_b0.append(quantize_weight(rounded_b))
+        w3raw01 = load_weight(w3, 0, 1)
+        w3raw11 = load_weight(w3, 1, 1)
+        x1b, x2b = make_x(picked1, azim1)
+        x1_ops.append(quantize_x("x1", x1b))
+        x2_ops.append(quantize_x("x2", x2b))
+
+        tanhs = {}
+
+        def tanh_product(b, t):
+            n0 = PASS * b + P * t
+            e1 = psum.tile([P, M], F32, name="e1_acc", bufs=2)
+            for a in range(PASSES):
+                nc.tensor.matmul_mx(
+                    out=e1[:],
+                    lhsT=w2_codes[:, a, 2 * n0 : 2 * (n0 + P)].bitcast(E2M1),
+                    lhsT_scale=w2_planes[:, a, n0 : n0 + P],
+                    rhs=x1_ops[a][0][:].bitcast(E4M3),
+                    rhs_scale=x1_ops[a][1][:],
+                    start=(a == 0),
+                    stop=(a == PASSES - 1),
+                )
+            tanh_e1 = ring.tile([P, M], F32, name="tanh_e1", bufs=8)
+            nc.scalar.activation(out=tanh_e1[:], in_=e1[:], func=ACT.Tanh)
+            tanhs[b, t] = tanh_e1
+
+        def products(w3_ops, b, t):
+            cols = slice(P * t, P * (t + 1))
+            e2 = psum.tile([P, M], F32, name="e2_acc", bufs=2)
+            for a in range(PASSES):
+                codes, plane = w3_ops[a]
+                nc.tensor.matmul_mx(
+                    out=e2[:],
+                    lhsT=codes[:, cols].bitcast(E4M3),
+                    lhsT_scale=plane[:, cols],
+                    rhs=x2_ops[a][0][:].bitcast(E4M3),
+                    rhs_scale=x2_ops[a][1][:],
+                    start=(a == 0),
+                    stop=(a == PASSES - 1),
+                )
+            turns_int = ring.tile([P, M], U32, name="turns_int")
+            turns = ring.tile([P, M], F32, name="turns")
+            angle = ring.tile([P, M], F32, name="angle")
+            tanh_e1 = tanhs[b, t]
+            nc.scalar.activation(
+                out=turns_int[:], in_=e2[:], func=ACT.Copy, scale=1.0 / (2.0 * math.pi), bias=ROUND_BIAS
+            )
+            nc.scalar.activation(out=turns[:], in_=turns_int[:], func=ACT.Copy, scale=1.0, bias=-ROUND_BIAS)
+            nc.vector.scalar_tensor_tensor(
+                out=angle[:], in0=turns[:], scalar=-2.0 * math.pi, in1=e2[:], op0=ALU.mult, op1=ALU.add
+            )
+            nc.scalar.activation(out=angle[:], in_=angle[:], func=ACT.Sin)
+            return tanh_e1, angle
+
+        def restore(parts, b, t):
+            tanh_e1, sin_e2 = parts
+            page = pages[b, t]
+            nc.vector.tensor_tensor(out=tanh_e1[:], in0=tanh_e1[:], in1=sin_e2[:], op=ALU.add)
+            nc.vector.tensor_tensor(page[:].indirect(error_list[:]), tanh_e1[:], wgo_rows[:, t, :], ALU.mult)
+            nc.sync.dma_start(out=out.rearrange("(b p t) j -> b t p j", p=P, t=PACK)[b, t], in_=page[:])
+
+        w3_ops = {0: w3_b0}
+        order = [(b, t) for b in range(PASSES) for t in range(PACK)]
+        waiting = None
+        for b, t in order:
+            tanh_product(b, t)
+        for i, (b, t) in enumerate(order):
+            parts = products(w3_ops[b], b, t)
+            if waiting is not None:
+                restore(*waiting)
+            waiting = (parts, b, t)
+            if i + 2 < len(order):
+                scale_page(*order[i + 2])
+            if i == 1:
+                w3_ops[1] = [quantize_weight(round_weight(w3raw01, nc.scalar.copy, 0, PACK))]
+            if i == 2:
+                w3_ops[1].append(quantize_weight(round_weight(w3raw11, nc.scalar.copy, 0, PACK)))
+        restore(*waiting)

@@ -40,84 +40,32 @@ def tile_list_soundtrack_slit_restorer_kernel(
         w2_scales_raw = keep.tile([P, PASSES, H], U8, name="w2_scales_raw", align_bytes=64)
         w2_raw = keep.tile([P, PASSES, 2 * H], U8, name="w2_raw", align_bytes=64)
         gain_sb = keep.tile([P, PASSES, PACK], F32, name="gain_sb")
-        skip_sb = keep.tile([P, PASSES, PACK], F32, name="skip_sb")
+        skip_sb = [keep.tile([P, PACK], F32, name=f"skip_sb{b}") for b in range(PASSES)]
+        zero_in = keep.tile([P, 1], F32, name="zero_in")
+        zero_bias = keep.tile([P, 1], F32, name="zero_bias")
 
-        nc.vector.memset(w2_scales_raw[:].rearrange("p a c -> p (a c)").bitcast(I32), 0)
         nc.vector.memset(table_scales[:].bitcast(I32), 0)
+        nc.vector.memset(w2_scales_raw[:].rearrange("p a c -> p (a c)").bitcast(I32), 0)
+        nc.vector.memset(zero_in[:], 0.0)
 
-        nc.sync.dma_start(slit_list[:], offs)
-        nc.sync.dma_start(out=w2_raw[:].bitcast(I32), in_=w2_words.rearrange("a p c -> p a c").bitcast(I32))
-        for q in range(4):
-            nc.scalar.dma_start(
-                out=w2_scales_raw[32 * q : 32 * q + 4, :, :].bitcast(I32),
-                in_=w2_scales[:, 4 * q : 4 * q + 4, :].rearrange("a r c -> r a c").bitcast(I32),
-            )
-        for q in range(4):
-            nc.scalar.dma_start(
-                out=table_scales[32 * q : 32 * q + 4 * PASSES, :].bitcast(I32),
-                in_=tab_scales[:, 4 * q : 4 * q + 4, :].bitcast(I32),
-            )
-        nc.scalar.dma_start(out=gain_sb[:], in_=gain.rearrange("(b p t) -> p b t", p=P, t=PACK))
-        nc.scalar.dma_start(out=skip_sb[:], in_=skip.rearrange("(b p t) -> p b t", p=P, t=PACK))
+        table = [keep.tile([P, T], I32, name=f"table{a}", align_bytes=64) for a in range(PASSES)]
+        pages = {}
 
-        table = []
-        for a in range(PASSES):
-            words = keep.tile([P, T], I32, name=f"table{a}", align_bytes=64)
-            nc.sync.dma_start(out=words[:], in_=tab_words[a].rearrange("p t i -> p (t i)").bitcast(I32))
-            table.append(words)
-        nc.sync.dma_start(error_list[:], pos1)
+        def load_table(a):
+            nc.sync.dma_start(out=table[a][:], in_=tab_words[a].rearrange("p t i -> p (t i)").bitcast(I32))
 
-        w2_codes = keep.tile([P, PASSES, 2 * H], U8, name="w2_codes", align_bytes=64)
-        w2_planes = keep.tile([P, PASSES, H], U8, name="w2_planes", align_bytes=64)
-        nc.vector.tensor_copy(
-            out=w2_codes[:].rearrange("p a c -> p (a c)").bitcast(U16).rearrange("p (g t q) -> p g q t", t=PACK, q=P),
-            in_=w2_raw[:].rearrange("p a c -> p (a c)").bitcast(U16).rearrange("p (g q t) -> p g q t", t=PACK, q=P),
-        )
-        nc.vector.tensor_copy(
-            out=w2_planes[:].rearrange("p a (b t q) -> p (a b) q t", t=PACK, q=P),
-            in_=w2_scales_raw[:].rearrange("p a (b q t) -> p (a b) q t", t=PACK, q=P),
-        )
-
-        kept_scale = keep.tile([P, PASSES, PACK], F32, name="kept_scale")
-        nc.vector.tensor_tensor(out=kept_scale[:], in0=gain_sb[:], in1=skip_sb[:], op=ALU.mult)
-
-        v_scales = keep.tile([P, S], U8, name="v_scales", align_bytes=64)
-        nc.vector.tensor_copy(v_scales[:], table_scales[:].indirect(slit_list[:]))
-        v_codes = []
-        for a in range(PASSES):
-            picked = keep.tile([P, S], U32, name=f"v_codes{a}", align_bytes=64)
-            nc.vector.tensor_copy(picked[:], table[a][:].bitcast(U32).indirect(slit_list[:]))
-            v_codes.append(picked)
+        def load_table_scales(a):
+            for q in range(4):
+                nc.sync.dma_start(
+                    out=table_scales[32 * q + 4 * a : 32 * q + 4 * a + 4, :].bitcast(I32),
+                    in_=tab_scales[a, 4 * q : 4 * q + 4, :].bitcast(I32),
+                )
 
         def load_weight(w, a, b):
-            raw = ring.tile([P, PACK, PASS], F32, name="w_raw", bufs=3)
+            raw = ring.tile([P, PACK, PASS], F32, name="w_raw", bufs=4, align_bytes=64)
             rows = w[PASS * a : PASS * (a + 1), PASS * b : PASS * (b + 1)]
             nc.sync.dma_start(out=raw[:], in_=rows.rearrange("(p j) c -> p j c", j=PACK))
             return raw
-
-        def round_weight(raw, copy, t0, t1):
-            rounded = ring.tile([P, t1 - t0, P, PACK], BF16, name="w_rounded", bufs=3, align_bytes=64)
-            copy(
-                out=rounded[:].rearrange("p t q j -> p q j t"),
-                in_=raw[:].rearrange("p j (q t) -> p q j t", t=PACK)[:, :, :, t0:t1],
-            )
-            return rounded
-
-        def new_operand(name, bufs):
-            codes = ring.tile([P, PASS], U32, name=name + "_codes", bufs=bufs, align_bytes=64)
-            plane = ring.tile([P, PASS], U8, name=name + "_plane", bufs=bufs, align_bytes=64)
-            return codes, plane
-
-        def quantize(operand, rounded, c0, c1):
-            codes, plane = operand
-            nc.vector.quantize_mx(out=codes[:, c0:c1].bitcast(E4M3), scales=plane[:, c0:c1], in_=rounded)
-
-        def quantize_weight(rounded):
-            operand = new_operand("w", 4)
-            quantize(operand, rounded[:].rearrange("p t q j -> p (t q j)"), 0, PASS)
-            return operand
-
-        pages = {}
 
         def load_density(b, t):
             page = keep.tile([P, S], F32, name=f"page{b}{t}")
@@ -125,18 +73,108 @@ def tile_list_soundtrack_slit_restorer_kernel(
             pages[b, t] = page
 
         def load_azim(b):
-            rows = ring.tile([P, PACK, M], F32, name="azim_rows", bufs=1)
+            rows = ring.tile([P, PACK, M], F32, name="azim_rows", bufs=2)
             nc.sync.dma_start(out=rows[:], in_=azim[PASS * b : PASS * (b + 1), :].rearrange("(p t) m -> p t m", t=PACK))
             return rows
 
-        def features(w1_ops, b, t):
+        def load_w2_scales():
+            for q in range(4):
+                nc.sync.dma_start(
+                    out=w2_scales_raw[32 * q : 32 * q + 4, :, :].bitcast(I32),
+                    in_=w2_scales[:, 4 * q : 4 * q + 4, :].rearrange("a r c -> r a c").bitcast(I32),
+                )
+
+        def load_skip(b):
+            nc.sync.dma_start(out=skip_sb[b][:], in_=skip.rearrange("(b p t) -> b p t", p=P, t=PACK)[b])
+
+        def load_wgo():
+            for q in range(4):
+                nc.sync.dma_start(out=wgo_rows[32 * q : 32 * (q + 1)], in_=wgo.rearrange("(p t) m -> p t m", t=PACK))
+
+        wgo_rows = keep.tile([P, PACK, M], F32, name="wgo_rows")
+        raw00 = load_weight(w1, 0, 0)
+        nc.sync.dma_start(slit_list[:], offs)
+        load_table_scales(0)
+        raw10 = load_weight(w1, 1, 0)
+        nc.sync.dma_start(out=w2_raw[:].bitcast(I32), in_=w2_words.rearrange("a p c -> p a c").bitcast(I32))
+        load_table_scales(1)
+        load_table(0)
+        nc.sync.dma_start(out=gain_sb[:], in_=gain.rearrange("(b p t) -> p b t", p=P, t=PACK))
+        load_w2_scales()
+        load_table(1)
+        nc.sync.dma_start(error_list[:], pos1)
+        load_density(0, 0)
+        load_density(0, 1)
+        raw01 = load_weight(w1, 0, 1)
+        load_density(0, 2)
+        raw11 = load_weight(w1, 1, 1)
+        load_skip(0)
+        load_density(0, 3)
+        load_density(1, 0)
+        azim0 = load_azim(0)
+        load_density(1, 1)
+        w3raw00 = load_weight(w3, 0, 0)
+        load_density(1, 2)
+        w3raw10 = load_weight(w3, 1, 0)
+        w3raw01 = load_weight(w3, 0, 1)
+        w3raw11 = load_weight(w3, 1, 1)
+        load_density(1, 3)
+        azim1 = load_azim(1)
+        load_wgo()
+        load_skip(1)
+        nc.scalar.activation(out=zero_bias[:], in_=zero_in[:], func=ACT.Silu)
+
+        def round_weight(raw, rounded):
+            nc.scalar.copy(
+                out=rounded[:].rearrange("p (t q j) -> p q j t", t=PACK, j=PACK),
+                in_=raw[:].rearrange("p j (q t) -> p q j t", t=PACK),
+            )
+
+        def quantize(name, bufs, rounded):
+            codes = ring.tile([P, PASS], U32, name=name + "_codes", bufs=bufs, align_bytes=64)
+            plane = ring.tile([P, PASS], U8, name=name + "_plane", bufs=bufs, align_bytes=64)
+            nc.vector.quantize_mx(out=codes[:].bitcast(E4M3), scales=plane[:], in_=rounded[:])
+            return codes, plane
+
+        stage = [keep.tile([P, PASS * PACK], BF16, name=f"stage{i}", align_bytes=64) for i in range(6)]
+
+        w2_codes = keep.tile([P, PASSES, 2 * H], U8, name="w2_codes", align_bytes=64)
+        w2_planes = keep.tile([P, PASSES, H], U8, name="w2_planes", align_bytes=64)
+        v_scales = keep.tile([P, S], U8, name="v_scales", align_bytes=64)
+        v_codes = [keep.tile([P, S], U32, name=f"v_codes{a}", align_bytes=64) for a in range(PASSES)]
+
+        round_weight(raw00, stage[0])
+        round_weight(raw10, stage[1])
+        w1_ops = {(0, 0): quantize("w", 4, stage[0])}
+        nc.vector.tensor_copy(v_scales[:], table_scales[:].indirect(slit_list[:]))
+        w1_ops[1, 0] = quantize("w", 4, stage[1])
+        nc.vector.tensor_copy(
+            out=w2_codes[:].rearrange("p a c -> p (a c)").bitcast(U16).rearrange("p (g t q) -> p g q t", t=PACK, q=P),
+            in_=w2_raw[:].rearrange("p a c -> p (a c)").bitcast(U16).rearrange("p (g q t) -> p g q t", t=PACK, q=P),
+        )
+        nc.vector.tensor_copy(v_codes[0][:], table[0][:].bitcast(U32).indirect(slit_list[:]))
+        nc.vector.tensor_copy(
+            out=w2_planes[:].rearrange("p a (b t q) -> p (a b) q t", t=PACK, q=P),
+            in_=w2_scales_raw[:].rearrange("p a (b q t) -> p (a b) q t", t=PACK, q=P),
+        )
+        for j0 in range(0, S, BANK):
+            nc.vector.tensor_copy(
+                v_codes[1][:, j0 : j0 + BANK],
+                table[1][:].bitcast(U32).indirect(slit_list[:, j0 // 16 : (j0 + BANK) // 16]),
+            )
+        kept_scale = [keep.tile([P, PACK], F32, name=f"kept_scale{b}") for b in range(PASSES)]
+
+        def make_kept_scale(b):
+            nc.gpsimd.tensor_tensor(out=kept_scale[b][:], in0=gain_sb[:, b, :], in1=skip_sb[b][:], op=ALU.mult)
+
+        def features(b, t):
             page = pages[b, t]
             cols = slice(P * t, P * (t + 1))
             for j0 in range(0, S, BANK):
                 slits = slice(j0, j0 + BANK)
                 acc = psum.tile([P, BANK], F32, name="feature_acc", bufs=4)
                 for a in range(PASSES):
-                    codes, plane = w1_ops[a]
+                    codes, plane = w1_ops[a, b]
                     nc.tensor.matmul_mx(
                         out=acc[:],
                         lhsT=codes[:, cols].bitcast(E4M3),
@@ -151,17 +189,21 @@ def tile_list_soundtrack_slit_restorer_kernel(
         def pick(picked, b, t):
             page = pages[b, t]
             nc.vector.tensor_copy(picked[:, t, :], page[:].indirect(error_list[:]))
-            nc.scalar.activation(
-                out=picked[:, t, :], in_=picked[:, t, :], func=ACT.Copy, scale=gain_sb[:, b, t : t + 1]
+            engine = nc.vector if (b, t) == (PASSES - 1, PACK - 1) else nc.gpsimd
+            engine.tensor_scalar(
+                out=picked[:, t, :],
+                in0=picked[:, t, :],
+                scalar1=gain_sb[:, b, t : t + 1],
+                scalar2=0.0,
+                op0=ALU.mult,
+                op1=ALU.add,
             )
 
         def scale_page(b, t):
             page = pages[b, t]
-            nc.scalar.activation(out=page[:], in_=page[:], func=ACT.Copy, scale=kept_scale[:, b, t : t + 1])
+            nc.scalar.activation(out=page[:], in_=page[:], func=ACT.Copy, scale=kept_scale[b][:, t : t + 1])
 
-        def make_x(picked, azim_rows):
-            x1 = ring.tile([P, M * PACK], BF16, name="x1_rounded", bufs=1, align_bytes=64)
-            x2 = ring.tile([P, M * PACK], BF16, name="x2_rounded", bufs=1, align_bytes=64)
+        def make_x(picked, azim_rows, x1, x2):
             src = picked[:].rearrange("p t (c i) -> p c t i", i=4)
             nc.scalar.copy(out=x1[:].rearrange("p (c i t) -> p c t i", i=4, t=PACK), in_=src)
             nc.vector.tensor_tensor(
@@ -170,81 +212,95 @@ def tile_list_soundtrack_slit_restorer_kernel(
                 in1=azim_rows[:].rearrange("p t (c i) -> p c t i", i=4),
                 op=ALU.mult,
             )
-            return x1, x2
 
-        def quantize_x(name, rounded):
-            operand = new_operand(name, 2)
-            quantize(operand, rounded[:], 0, M)
-            return operand
-
-        raw00 = load_weight(w1, 0, 0)
-        raw10 = load_weight(w1, 1, 0)
-        load_density(0, 0)
-        load_density(0, 1)
-        raw01 = load_weight(w1, 0, 1)
-        load_density(0, 2)
-        w1_b0 = [quantize_weight(round_weight(raw00, nc.scalar.copy, 0, PACK))]
-        last = new_operand("w", 4)
-        low = round_weight(raw10, nc.vector.tensor_copy, 0, 2)
-        high = round_weight(raw10, nc.scalar.copy, 2, 4)
-        quantize(last, low[:].rearrange("p t q j -> p (t q j)"), 0, 2 * P)
-        quantize(last, high[:].rearrange("p t q j -> p (t q j)"), 2 * P, 4 * P)
-        w1_b0.append(last)
-        raw11 = load_weight(w1, 1, 1)
-        load_density(0, 3)
-        azim0 = load_azim(0)
-        for t in range(PACK):
-            load_density(1, t)
-
+        w3_ops = {}
         picked0 = ring.tile([P, PACK, M], F32, name="picked")
-        features(w1_b0, 0, 0)
-        features(w1_b0, 0, 1)
-        pick(picked0, 0, 0)
-        rounded01 = round_weight(raw01, nc.scalar.copy, 0, PACK)
-        features(w1_b0, 0, 2)
-        pick(picked0, 0, 1)
-        rounded11 = round_weight(raw11, nc.scalar.copy, 0, PACK)
-        features(w1_b0, 0, 3)
-        w1_b1 = [quantize_weight(rounded01)]
-        pick(picked0, 0, 2)
-        w1_b1.append(quantize_weight(rounded11))
-        pick(picked0, 0, 3)
-        w3raw00 = load_weight(w3, 0, 0)
-        w3raw10 = load_weight(w3, 1, 0)
-
         picked1 = ring.tile([P, PACK, M], F32, name="picked")
-        features(w1_b1, 1, 0)
-        x1a, x2a = make_x(picked0, azim0)
-        azim1 = load_azim(1)
-        wgo_rows = keep.tile([P, PACK, M], F32, name="wgo_rows")
-        for q in range(4):
-            nc.sync.dma_start(out=wgo_rows[32 * q : 32 * (q + 1)], in_=wgo.rearrange("(p t) m -> p t m", t=PACK))
-        features(w1_b1, 1, 1)
+        features(0, 0)
+        round_weight(raw01, stage[2])
+        features(0, 1)
+        pick(picked0, 0, 0)
+        round_weight(raw11, stage[3])
+        features(0, 2)
+        pick(picked0, 0, 1)
+        w1_ops[0, 1] = quantize("w", 4, stage[2])
+        make_kept_scale(0)
+        features(0, 3)
+        pick(picked0, 0, 2)
+        w1_ops[1, 1] = quantize("w", 4, stage[3])
+        pick(picked0, 0, 3)
+        features(1, 0)
+        make_x(picked0, azim0, stage[0], stage[1])
+        features(1, 1)
         pick(picked1, 1, 0)
-        x2_ops = [quantize_x("x2", x2a)]
-        x1_ops = [quantize_x("x1", x1a)]
+        x2_ops = [quantize("x2", 2, stage[1])]
+        x1_ops = [quantize("x1", 2, stage[0])]
+        round_weight(w3raw00, stage[2])
         scale_page(0, 0)
-        scale_page(0, 1)
-        features(w1_b1, 1, 2)
+        features(1, 2)
         pick(picked1, 1, 1)
-        rounded_a = round_weight(w3raw00, nc.scalar.copy, 0, PACK)
-        features(w1_b1, 1, 3)
+        round_weight(w3raw10, stage[3])
+        scale_page(0, 1)
+        features(1, 3)
+        w3_ops[0, 0] = quantize("w", 4, stage[2])
+        round_weight(w3raw01, stage[4])
         pick(picked1, 1, 2)
-        rounded_b = round_weight(w3raw10, nc.scalar.copy, 0, PACK)
-        w3_b0 = [quantize_weight(rounded_a)]
+        round_weight(w3raw11, stage[5])
+        scale_page(0, 2)
+        scale_page(0, 3)
         pick(picked1, 1, 3)
-        w3_b0.append(quantize_weight(rounded_b))
-        w3raw01 = load_weight(w3, 0, 1)
-        w3raw11 = load_weight(w3, 1, 1)
-        x1b, x2b = make_x(picked1, azim1)
-        x1_ops.append(quantize_x("x1", x1b))
-        x2_ops.append(quantize_x("x2", x2b))
+        w3_ops[1, 0] = quantize("w", 4, stage[3])
+        make_x(picked1, azim1, stage[0], stage[1])
+        x2_ops.append(quantize("x2", 2, stage[1]))
+        x1_ops.append(quantize("x1", 2, stage[0]))
+        w3_ops[0, 1] = quantize("w", 4, stage[4])
+        w3_ops[1, 1] = quantize("w", 4, stage[5])
+        make_kept_scale(1)
 
-        tanhs = {}
+        first_int = keep.tile([P, M], I32, name="first_int")
+
+        def sine_angle(b, t):
+            cols = slice(P * t, P * (t + 1))
+            e2 = psum.tile([P, M], F32, name="product_acc", bufs=4)
+            for a in range(PASSES):
+                codes, plane = w3_ops[a, b]
+                nc.tensor.matmul_mx(
+                    out=e2[:],
+                    lhsT=codes[:, cols].bitcast(E4M3),
+                    lhsT_scale=plane[:, cols],
+                    rhs=x2_ops[a][0][:].bitcast(E4M3),
+                    rhs_scale=x2_ops[a][1][:],
+                    start=(a == 0),
+                    stop=(a == PASSES - 1),
+                )
+            turns = ring.tile([P, M], F32, name="turns")
+            angle = ring.tile([P, M], F32, name="angle", bufs=3)
+            if (b, t) == (0, 0):
+                nc.vector.tensor_scalar(
+                    out=first_int[:],
+                    in0=e2[:],
+                    scalar1=1.0 / (2.0 * math.pi),
+                    scalar2=ROUND_BIAS,
+                    op0=ALU.mult,
+                    op1=ALU.add,
+                )
+                nc.vector.tensor_scalar(
+                    out=turns[:], in0=first_int[:], scalar1=-ROUND_BIAS, scalar2=None, op0=ALU.add
+                )
+            else:
+                turns_int = ring.tile([P, M], U32, name="turns_int", bufs=1)
+                nc.scalar.activation(
+                    out=turns_int[:], in_=e2[:], func=ACT.Copy, scale=1.0 / (2.0 * math.pi), bias=ROUND_BIAS
+                )
+                nc.scalar.activation(out=turns[:], in_=turns_int[:], func=ACT.Copy, scale=1.0, bias=-ROUND_BIAS)
+            nc.vector.scalar_tensor_tensor(
+                out=angle[:], in0=turns[:], scalar=-2.0 * math.pi, in1=e2[:], op0=ALU.mult, op1=ALU.add
+            )
+            return angle
 
         def tanh_product(b, t):
             n0 = PASS * b + P * t
-            e1 = psum.tile([P, M], F32, name="e1_acc", bufs=2)
+            e1 = psum.tile([P, M], F32, name="product_acc", bufs=4)
             for a in range(PASSES):
                 nc.tensor.matmul_mx(
                     out=e1[:],
@@ -255,59 +311,31 @@ def tile_list_soundtrack_slit_restorer_kernel(
                     start=(a == 0),
                     stop=(a == PASSES - 1),
                 )
-            tanh_e1 = ring.tile([P, M], F32, name="tanh_e1", bufs=8)
-            nc.scalar.activation(out=tanh_e1[:], in_=e1[:], func=ACT.Tanh)
-            tanhs[b, t] = tanh_e1
+            tanh_e1 = ring.tile([P, M], F32, name="tanh_e1", bufs=2)
+            nc.scalar.activation(out=tanh_e1[:], in_=e1[:], func=ACT.Tanh, bias=zero_bias[:])
+            return tanh_e1
 
-        def products(w3_ops, b, t):
-            cols = slice(P * t, P * (t + 1))
-            e2 = psum.tile([P, M], F32, name="e2_acc", bufs=2)
-            for a in range(PASSES):
-                codes, plane = w3_ops[a]
-                nc.tensor.matmul_mx(
-                    out=e2[:],
-                    lhsT=codes[:, cols].bitcast(E4M3),
-                    lhsT_scale=plane[:, cols],
-                    rhs=x2_ops[a][0][:].bitcast(E4M3),
-                    rhs_scale=x2_ops[a][1][:],
-                    start=(a == 0),
-                    stop=(a == PASSES - 1),
-                )
-            turns_int = ring.tile([P, M], U32, name="turns_int")
-            turns = ring.tile([P, M], F32, name="turns")
-            angle = ring.tile([P, M], F32, name="angle")
-            tanh_e1 = tanhs[b, t]
-            nc.scalar.activation(
-                out=turns_int[:], in_=e2[:], func=ACT.Copy, scale=1.0 / (2.0 * math.pi), bias=ROUND_BIAS
-            )
-            nc.scalar.activation(out=turns[:], in_=turns_int[:], func=ACT.Copy, scale=1.0, bias=-ROUND_BIAS)
-            nc.vector.scalar_tensor_tensor(
-                out=angle[:], in0=turns[:], scalar=-2.0 * math.pi, in1=e2[:], op0=ALU.mult, op1=ALU.add
-            )
-            nc.scalar.activation(out=angle[:], in_=angle[:], func=ACT.Sin)
-            return tanh_e1, angle
-
-        def restore(parts, b, t):
-            tanh_e1, sin_e2 = parts
+        def restore(tanh_e1, angle, b, t):
             page = pages[b, t]
-            nc.vector.tensor_tensor(out=tanh_e1[:], in0=tanh_e1[:], in1=sin_e2[:], op=ALU.add)
-            nc.vector.tensor_tensor(page[:].indirect(error_list[:]), tanh_e1[:], wgo_rows[:, t, :], ALU.mult)
+            nc.scalar.activation(out=angle[:], in_=angle[:], func=ACT.Sin, bias=zero_bias[:])
+            if b == 0 and t < 1:
+                nc.vector.tensor_tensor(out=angle[:], in0=tanh_e1[:], in1=angle[:], op=ALU.add)
+                nc.vector.tensor_tensor(out=angle[:], in0=angle[:], in1=wgo_rows[:, t, :], op=ALU.mult)
+            else:
+                total = ring.tile([P, M], F32, name="total", bufs=1)
+                nc.gpsimd.tensor_tensor(out=total[:], in0=tanh_e1[:], in1=angle[:], op=ALU.add)
+                nc.gpsimd.tensor_tensor(out=angle[:], in0=total[:], in1=wgo_rows[:, t, :], op=ALU.mult)
+            nc.vector.tensor_copy(page[:].indirect(error_list[:]), angle[:])
             nc.sync.dma_start(out=out.rearrange("(b p t) j -> b t p j", p=P, t=PACK)[b, t], in_=page[:])
 
-        w3_ops = {0: w3_b0}
         order = [(b, t) for b in range(PASSES) for t in range(PACK)]
-        waiting = None
-        for b, t in order:
-            tanh_product(b, t)
+        angles = [sine_angle(0, 0)]
         for i, (b, t) in enumerate(order):
-            parts = products(w3_ops[b], b, t)
-            if waiting is not None:
-                restore(*waiting)
-            waiting = (parts, b, t)
+            tanh_e1 = tanh_product(b, t)
+            if i == 0:
+                angles.append(sine_angle(*order[1]))
+            restore(tanh_e1, angles[i], b, t)
             if i + 2 < len(order):
-                scale_page(*order[i + 2])
-            if i == 1:
-                w3_ops[1] = [quantize_weight(round_weight(w3raw01, nc.scalar.copy, 0, PACK))]
-            if i == 2:
-                w3_ops[1].append(quantize_weight(round_weight(w3raw11, nc.scalar.copy, 0, PACK)))
-        restore(*waiting)
+                angles.append(sine_angle(*order[i + 2]))
+            if 1 <= i < 5:
+                scale_page(1, i - 1)

@@ -2,6 +2,7 @@ import math
 from contextlib import ExitStack
 
 import concourse.mybir as mybir
+from concourse.masks import make_identity
 
 K, H, T, S, M = 1024, 1024, 4096, 1024, 512
 FLOPS = 2 * K * H * S + 2 * 2 * H * H * M
@@ -40,7 +41,8 @@ def tile_list_soundtrack_slit_restorer_kernel(
         w2_scales_raw = keep.tile([P, PASSES, H], U8, name="w2_scales_raw", align_bytes=64)
         w2_raw = keep.tile([P, PASSES, 2 * H], U8, name="w2_raw", align_bytes=64)
         gain_sb = keep.tile([P, PASSES, PACK], F32, name="gain_sb")
-        skip_sb = [keep.tile([P, PACK], F32, name=f"skip_sb{b}") for b in range(PASSES)]
+        skip_parts = [(0, 0, 2), (0, 2, 4), (1, 0, 4)]
+        skip_sb = [keep.tile([P, t1 - t0], F32, name=f"skip_sb{b}{t0}") for b, t0, t1 in skip_parts]
         zero_in = keep.tile([P, 1], F32, name="zero_in")
         zero_bias = keep.tile([P, 1], F32, name="zero_bias")
 
@@ -54,15 +56,15 @@ def tile_list_soundtrack_slit_restorer_kernel(
         def load_table(a):
             nc.sync.dma_start(out=table[a][:], in_=tab_words[a].rearrange("p t i -> p (t i)").bitcast(I32))
 
-        def load_table_scales(a):
+        def load_table_scales():
             for q in range(4):
                 nc.sync.dma_start(
-                    out=table_scales[32 * q + 4 * a : 32 * q + 4 * a + 4, :].bitcast(I32),
-                    in_=tab_scales[a, 4 * q : 4 * q + 4, :].bitcast(I32),
+                    out=table_scales[32 * q : 32 * q + 4 * PASSES, :].bitcast(I32),
+                    in_=tab_scales[:, 4 * q : 4 * q + 4, :].bitcast(I32),
                 )
 
         def load_weight(w, a, b):
-            raw = ring.tile([P, PACK, PASS], F32, name="w_raw", bufs=4, align_bytes=64)
+            raw = ring.tile([P, PACK, PASS], F32, name="w_raw", bufs=5, align_bytes=64)
             rows = w[PASS * a : PASS * (a + 1), PASS * b : PASS * (b + 1)]
             nc.sync.dma_start(out=raw[:], in_=rows.rearrange("(p j) c -> p j c", j=PACK))
             return raw
@@ -84,23 +86,21 @@ def tile_list_soundtrack_slit_restorer_kernel(
                     in_=w2_scales[:, 4 * q : 4 * q + 4, :].rearrange("a r c -> r a c").bitcast(I32),
                 )
 
-        def load_skip(b):
-            nc.sync.dma_start(out=skip_sb[b][:], in_=skip.rearrange("(b p t) -> b p t", p=P, t=PACK)[b])
+        def load_skip(part):
+            b, t0, t1 = skip_parts[part]
+            nc.sync.dma_start(out=skip_sb[part][:], in_=skip.rearrange("(b p t) -> b p t", p=P, t=PACK)[b, :, t0:t1])
 
-        def load_wgo():
-            for q in range(4):
-                nc.sync.dma_start(out=wgo_rows[32 * q : 32 * (q + 1)], in_=wgo.rearrange("(p t) m -> p t m", t=PACK))
-
+        wgo_plain = ring.tile([P, M], F32, name="turns")
         wgo_rows = keep.tile([P, PACK, M], F32, name="wgo_rows")
-        raw00 = load_weight(w1, 0, 0)
         nc.sync.dma_start(slit_list[:], offs)
-        load_table_scales(0)
-        raw10 = load_weight(w1, 1, 0)
         nc.sync.dma_start(out=w2_raw[:].bitcast(I32), in_=w2_words.rearrange("a p c -> p a c").bitcast(I32))
-        load_table_scales(1)
+        load_table_scales()
+        load_w2_scales()
+        raw00 = load_weight(w1, 0, 0)
+        raw10 = load_weight(w1, 1, 0)
+        nc.sync.dma_start(out=wgo_plain[:], in_=wgo)
         load_table(0)
         nc.sync.dma_start(out=gain_sb[:], in_=gain.rearrange("(b p t) -> p b t", p=P, t=PACK))
-        load_w2_scales()
         load_table(1)
         nc.sync.dma_start(error_list[:], pos1)
         load_density(0, 0)
@@ -117,11 +117,11 @@ def tile_list_soundtrack_slit_restorer_kernel(
         load_density(1, 2)
         w3raw10 = load_weight(w3, 1, 0)
         w3raw01 = load_weight(w3, 0, 1)
-        w3raw11 = load_weight(w3, 1, 1)
         load_density(1, 3)
         azim1 = load_azim(1)
-        load_wgo()
+        w3raw11 = load_weight(w3, 1, 1)
         load_skip(1)
+        load_skip(2)
         nc.scalar.activation(out=zero_bias[:], in_=zero_in[:], func=ACT.Silu)
 
         def round_weight(raw, rounded):
@@ -136,7 +136,7 @@ def tile_list_soundtrack_slit_restorer_kernel(
             nc.vector.quantize_mx(out=codes[:].bitcast(E4M3), scales=plane[:], in_=rounded[:])
             return codes, plane
 
-        stage = [keep.tile([P, PASS * PACK], BF16, name=f"stage{i}", align_bytes=64) for i in range(6)]
+        stage = [keep.tile([P, PASS * PACK], BF16, name=f"stage{i}", align_bytes=64) for i in range(5)]
 
         w2_codes = keep.tile([P, PASSES, 2 * H], U8, name="w2_codes", align_bytes=64)
         w2_planes = keep.tile([P, PASSES, H], U8, name="w2_planes", align_bytes=64)
@@ -162,10 +162,28 @@ def tile_list_soundtrack_slit_restorer_kernel(
                 v_codes[1][:, j0 : j0 + BANK],
                 table[1][:].bitcast(U32).indirect(slit_list[:, j0 // 16 : (j0 + BANK) // 16]),
             )
-        kept_scale = [keep.tile([P, PACK], F32, name=f"kept_scale{b}") for b in range(PASSES)]
+        identity = keep.tile([P, P], F32, name="identity")
+        make_identity(nc, identity[:])
+        turned = psum.tile([P, PACK, P], F32, name="product_acc", bufs=4)
+        for c in range(PACK):
+            nc.tensor.transpose(turned[:, c, :], wgo_plain[:, P * c : P * (c + 1)], identity[:])
+        dealt = ring.tile([P, PACK, PACK, PACK, 32], F32, name="picked")
+        for q in range(PACK):
+            nc.scalar.copy(out=dealt[:, :, :, q, :], in_=turned[:].rearrange("m c (r t) -> m c t r", t=PACK))
+        for t in range(PACK):
+            back = psum.tile([P, PACK, P], F32, name="product_acc", bufs=4)
+            for c in range(PACK):
+                nc.tensor.transpose(back[:, c, :], dealt[:, c, t].rearrange("m q r -> m (q r)"), identity[:])
+            nc.scalar.copy(out=wgo_rows[:, t, :], in_=back[:].rearrange("p c m -> p (c m)"))
 
-        def make_kept_scale(b):
-            nc.gpsimd.tensor_tensor(out=kept_scale[b][:], in0=gain_sb[:, b, :], in1=skip_sb[b][:], op=ALU.mult)
+        kept_scale = {}
+
+        def make_kept_scale(part):
+            b, t0, t1 = skip_parts[part]
+            product = keep.tile([P, t1 - t0], F32, name=f"kept_scale{part}")
+            nc.gpsimd.tensor_tensor(out=product[:], in0=gain_sb[:, b, t0:t1], in1=skip_sb[part][:], op=ALU.mult)
+            for t in range(t0, t1):
+                kept_scale[b, t] = product[:, t - t0 : t - t0 + 1]
 
         def features(b, t):
             page = pages[b, t]
@@ -186,22 +204,20 @@ def tile_list_soundtrack_slit_restorer_kernel(
                     )
                 nc.vector.tensor_tensor(out=page[:, slits], in0=acc[:], in1=page[:, slits], op=ALU.max)
 
-        def pick(picked, b, t):
+        def pick(picked, scaled, b, t):
             page = pages[b, t]
             nc.vector.tensor_copy(picked[:, t, :], page[:].indirect(error_list[:]))
-            engine = nc.vector if (b, t) == (PASSES - 1, PACK - 1) else nc.gpsimd
-            engine.tensor_scalar(
-                out=picked[:, t, :],
-                in0=picked[:, t, :],
-                scalar1=gain_sb[:, b, t : t + 1],
-                scalar2=0.0,
-                op0=ALU.mult,
-                op1=ALU.add,
-            )
+            column = gain_sb[:, b, t : t + 1]
+            if (b, t) == (PASSES - 1, PACK - 1):
+                nc.vector.tensor_scalar(
+                    out=scaled[:, t, :], in0=picked[:, t, :], scalar1=column, scalar2=None, op0=ALU.mult
+                )
+            else:
+                nc.scalar.activation(out=scaled[:, t, :], in_=picked[:, t, :], func=ACT.Copy, scale=column)
 
         def scale_page(b, t):
             page = pages[b, t]
-            nc.scalar.activation(out=page[:], in_=page[:], func=ACT.Copy, scale=kept_scale[b][:, t : t + 1])
+            nc.scalar.activation(out=page[:], in_=page[:], func=ACT.Copy, scale=kept_scale[b, t])
 
         def make_x(picked, azim_rows, x1, x2):
             src = picked[:].rearrange("p t (c i) -> p c t i", i=4)
@@ -219,43 +235,42 @@ def tile_list_soundtrack_slit_restorer_kernel(
         features(0, 0)
         round_weight(raw01, stage[2])
         features(0, 1)
-        pick(picked0, 0, 0)
         round_weight(raw11, stage[3])
+        pick(picked0, raw11, 0, 0)
         features(0, 2)
-        pick(picked0, 0, 1)
+        pick(picked0, raw11, 0, 1)
         w1_ops[0, 1] = quantize("w", 4, stage[2])
         make_kept_scale(0)
         features(0, 3)
-        pick(picked0, 0, 2)
+        pick(picked0, raw11, 0, 2)
         w1_ops[1, 1] = quantize("w", 4, stage[3])
-        pick(picked0, 0, 3)
+        pick(picked0, raw11, 0, 3)
         features(1, 0)
-        make_x(picked0, azim0, stage[0], stage[1])
+        make_x(raw11, azim0, stage[0], stage[1])
         features(1, 1)
-        pick(picked1, 1, 0)
+        round_weight(w3raw00, stage[2])
+        round_weight(w3raw10, stage[3])
+        round_weight(w3raw01, stage[4])
+        pick(picked1, w3raw01, 1, 0)
         x2_ops = [quantize("x2", 2, stage[1])]
         x1_ops = [quantize("x1", 2, stage[0])]
-        round_weight(w3raw00, stage[2])
         scale_page(0, 0)
         features(1, 2)
-        pick(picked1, 1, 1)
-        round_weight(w3raw10, stage[3])
+        pick(picked1, w3raw01, 1, 1)
         scale_page(0, 1)
         features(1, 3)
         w3_ops[0, 0] = quantize("w", 4, stage[2])
-        round_weight(w3raw01, stage[4])
-        pick(picked1, 1, 2)
-        round_weight(w3raw11, stage[5])
-        scale_page(0, 2)
-        scale_page(0, 3)
-        pick(picked1, 1, 3)
+        pick(picked1, w3raw01, 1, 2)
+        pick(picked1, w3raw01, 1, 3)
         w3_ops[1, 0] = quantize("w", 4, stage[3])
-        make_x(picked1, azim1, stage[0], stage[1])
+        make_x(w3raw01, azim1, stage[0], stage[1])
         x2_ops.append(quantize("x2", 2, stage[1]))
         x1_ops.append(quantize("x1", 2, stage[0]))
         w3_ops[0, 1] = quantize("w", 4, stage[4])
-        w3_ops[1, 1] = quantize("w", 4, stage[5])
+        round_weight(w3raw11, stage[2])
+        w3_ops[1, 1] = quantize("w", 4, stage[2])
         make_kept_scale(1)
+        make_kept_scale(2)
 
         first_int = keep.tile([P, M], I32, name="first_int")
 
@@ -337,5 +352,5 @@ def tile_list_soundtrack_slit_restorer_kernel(
             restore(tanh_e1, angles[i], b, t)
             if i + 2 < len(order):
                 angles.append(sine_angle(*order[i + 2]))
-            if 1 <= i < 5:
-                scale_page(1, i - 1)
+            if 1 <= i < len(order) - 1:
+                scale_page(*order[i + 1])

import math
from contextlib import ExitStack

import concourse.mybir as mybir
from concourse.masks import make_identity

K, H, T, S, M = 1024, 1024, 4096, 1024, 512
FLOPS = 2 * K * H * S + 2 * 2 * H * H * M

F32 = mybir.dt.float32
BF16 = mybir.dt.bfloat16
I32 = mybir.dt.int32
U32 = mybir.dt.uint32
U16 = mybir.dt.uint16
U8 = mybir.dt.uint8
E4M3 = mybir.dt.float8_e4m3fn_x4
E2M1 = mybir.dt.float4_e2m1fn_x4
ALU = mybir.AluOpType
ACT = mybir.ActivationFunctionType

P = 128
PACK = 4
PASS = P * PACK
PASSES = 2
BANK = 512
ROUND_BIAS = 1.5 * 2.0**23


def tile_list_soundtrack_slit_restorer_kernel(
    tc, tab_words, tab_scales, offs, pos1, w1, density, gain, w2_words, w2_scales, azim, w3, skip, wgo, out
):
    nc = tc.nc
    with ExitStack() as ctx:
        keep = ctx.enter_context(tc.tile_pool(name="keep", bufs=1))
        ring = ctx.enter_context(tc.tile_pool(name="ring", bufs=2))
        psum = ctx.enter_context(tc.psum_pool(name="psum", bufs=1))

        slit_list = keep.tile([P, S // 16], U16, name="slit_list")
        error_list = keep.tile([P, M // 16], U16, name="error_list")
        table_scales = keep.tile([P, T], U8, name="table_scales", align_bytes=64)
        w2_scales_raw = keep.tile([P, PASSES, H], U8, name="w2_scales_raw", align_bytes=64)
        w2_raw = keep.tile([P, PASSES, 2 * H], U8, name="w2_raw", align_bytes=64)
        gain_sb = keep.tile([P, PASSES, PACK], F32, name="gain_sb")
        skip_parts = [(0, 0, 2), (0, 2, 4), (1, 0, 4)]
        skip_sb = [keep.tile([P, t1 - t0], F32, name=f"skip_sb{b}{t0}") for b, t0, t1 in skip_parts]
        zero_in = keep.tile([P, 1], F32, name="zero_in")
        zero_bias = keep.tile([P, 1], F32, name="zero_bias")

        nc.vector.memset(table_scales[:].bitcast(I32), 0)
        nc.vector.memset(w2_scales_raw[:].rearrange("p a c -> p (a c)").bitcast(I32), 0)
        nc.vector.memset(zero_in[:], 0.0)

        table = [keep.tile([P, T], I32, name=f"table{a}", align_bytes=64) for a in range(PASSES)]
        pages = {}

        def load_table(a):
            nc.sync.dma_start(out=table[a][:], in_=tab_words[a].rearrange("p t i -> p (t i)").bitcast(I32))

        def load_table_scales():
            for q in range(4):
                nc.sync.dma_start(
                    out=table_scales[32 * q : 32 * q + 4 * PASSES, :].bitcast(I32),
                    in_=tab_scales[:, 4 * q : 4 * q + 4, :].bitcast(I32),
                )

        def load_weight(w, a, b):
            raw = ring.tile([P, PACK, PASS], F32, name="w_raw", bufs=5, align_bytes=64)
            rows = w[PASS * a : PASS * (a + 1), PASS * b : PASS * (b + 1)]
            nc.sync.dma_start(out=raw[:], in_=rows.rearrange("(p j) c -> p j c", j=PACK))
            return raw

        def load_density(b, t):
            page = keep.tile([P, S], F32, name=f"page{b}{t}")
            nc.sync.dma_start(out=page[:], in_=density.rearrange("(b p t) j -> b t p j", p=P, t=PACK)[b, t])
            pages[b, t] = page

        def load_azim(b):
            rows = ring.tile([P, PACK, M], F32, name="azim_rows", bufs=2)
            nc.sync.dma_start(out=rows[:], in_=azim[PASS * b : PASS * (b + 1), :].rearrange("(p t) m -> p t m", t=PACK))
            return rows

        def load_w2_scales():
            for q in range(4):
                nc.sync.dma_start(
                    out=w2_scales_raw[32 * q : 32 * q + 4, :, :].bitcast(I32),
                    in_=w2_scales[:, 4 * q : 4 * q + 4, :].rearrange("a r c -> r a c").bitcast(I32),
                )

        def load_skip(part):
            b, t0, t1 = skip_parts[part]
            nc.sync.dma_start(out=skip_sb[part][:], in_=skip.rearrange("(b p t) -> b p t", p=P, t=PACK)[b, :, t0:t1])

        wgo_plain = ring.tile([P, M], F32, name="turns")
        wgo_rows = keep.tile([P, PACK, M], F32, name="wgo_rows")
        nc.sync.dma_start(slit_list[:], offs)
        nc.sync.dma_start(out=w2_raw[:].bitcast(I32), in_=w2_words.rearrange("a p c -> p a c").bitcast(I32))
        load_table_scales()
        load_w2_scales()
        raw00 = load_weight(w1, 0, 0)
        raw10 = load_weight(w1, 1, 0)
        nc.sync.dma_start(out=wgo_plain[:], in_=wgo)
        load_table(0)
        nc.sync.dma_start(out=gain_sb[:], in_=gain.rearrange("(b p t) -> p b t", p=P, t=PACK))
        load_table(1)
        nc.sync.dma_start(error_list[:], pos1)
        load_density(0, 0)
        load_density(0, 1)
        raw01 = load_weight(w1, 0, 1)
        load_density(0, 2)
        raw11 = load_weight(w1, 1, 1)
        load_skip(0)
        load_density(0, 3)
        load_density(1, 0)
        azim0 = load_azim(0)
        load_density(1, 1)
        w3raw00 = load_weight(w3, 0, 0)
        load_density(1, 2)
        w3raw10 = load_weight(w3, 1, 0)
        w3raw01 = load_weight(w3, 0, 1)
        load_density(1, 3)
        azim1 = load_azim(1)
        w3raw11 = load_weight(w3, 1, 1)
        load_skip(1)
        load_skip(2)
        nc.scalar.activation(out=zero_bias[:], in_=zero_in[:], func=ACT.Silu)

        def round_weight(raw, rounded):
            nc.scalar.copy(
                out=rounded[:].rearrange("p (t q j) -> p q j t", t=PACK, j=PACK),
                in_=raw[:].rearrange("p j (q t) -> p q j t", t=PACK),
            )

        def quantize(name, bufs, rounded):
            codes = ring.tile([P, PASS], U32, name=name + "_codes", bufs=bufs, align_bytes=64)
            plane = ring.tile([P, PASS], U8, name=name + "_plane", bufs=bufs, align_bytes=64)
            nc.vector.quantize_mx(out=codes[:].bitcast(E4M3), scales=plane[:], in_=rounded[:])
            return codes, plane

        stage = [keep.tile([P, PASS * PACK], BF16, name=f"stage{i}", align_bytes=64) for i in range(5)]

        w2_codes = keep.tile([P, PASSES, 2 * H], U8, name="w2_codes", align_bytes=64)
        w2_planes = keep.tile([P, PASSES, H], U8, name="w2_planes", align_bytes=64)
        v_scales = keep.tile([P, S], U8, name="v_scales", align_bytes=64)
        v_codes = [keep.tile([P, S], U32, name=f"v_codes{a}", align_bytes=64) for a in range(PASSES)]

        round_weight(raw00, stage[0])
        round_weight(raw10, stage[1])
        w1_ops = {(0, 0): quantize("w", 4, stage[0])}
        nc.vector.tensor_copy(v_scales[:], table_scales[:].indirect(slit_list[:]))
        w1_ops[1, 0] = quantize("w", 4, stage[1])
        nc.vector.tensor_copy(
            out=w2_codes[:].rearrange("p a c -> p (a c)").bitcast(U16).rearrange("p (g t q) -> p g q t", t=PACK, q=P),
            in_=w2_raw[:].rearrange("p a c -> p (a c)").bitcast(U16).rearrange("p (g q t) -> p g q t", t=PACK, q=P),
        )
        nc.vector.tensor_copy(v_codes[0][:], table[0][:].bitcast(U32).indirect(slit_list[:]))
        nc.vector.tensor_copy(
            out=w2_planes[:].rearrange("p a (b t q) -> p (a b) q t", t=PACK, q=P),
            in_=w2_scales_raw[:].rearrange("p a (b q t) -> p (a b) q t", t=PACK, q=P),
        )
        for j0 in range(0, S, BANK):
            nc.vector.tensor_copy(
                v_codes[1][:, j0 : j0 + BANK],
                table[1][:].bitcast(U32).indirect(slit_list[:, j0 // 16 : (j0 + BANK) // 16]),
            )
        identity = keep.tile([P, P], F32, name="identity")
        make_identity(nc, identity[:])
        turned = psum.tile([P, PACK, P], F32, name="product_acc", bufs=4)
        for c in range(PACK):
            nc.tensor.transpose(turned[:, c, :], wgo_plain[:, P * c : P * (c + 1)], identity[:])
        dealt = ring.tile([P, PACK, PACK, PACK, 32], F32, name="picked")
        for q in range(PACK):
            nc.scalar.copy(out=dealt[:, :, :, q, :], in_=turned[:].rearrange("m c (r t) -> m c t r", t=PACK))
        for t in range(PACK):
            back = psum.tile([P, PACK, P], F32, name="product_acc", bufs=4)
            for c in range(PACK):
                nc.tensor.transpose(back[:, c, :], dealt[:, c, t].rearrange("m q r -> m (q r)"), identity[:])
            nc.scalar.copy(out=wgo_rows[:, t, :], in_=back[:].rearrange("p c m -> p (c m)"))

        kept_scale = {}

        def make_kept_scale(part):
            b, t0, t1 = skip_parts[part]
            product = keep.tile([P, t1 - t0], F32, name=f"kept_scale{part}")
            nc.gpsimd.tensor_tensor(out=product[:], in0=gain_sb[:, b, t0:t1], in1=skip_sb[part][:], op=ALU.mult)
            for t in range(t0, t1):
                kept_scale[b, t] = product[:, t - t0 : t - t0 + 1]

        def features(b, t):
            page = pages[b, t]
            cols = slice(P * t, P * (t + 1))
            for j0 in range(0, S, BANK):
                slits = slice(j0, j0 + BANK)
                acc = psum.tile([P, BANK], F32, name="feature_acc", bufs=4)
                for a in range(PASSES):
                    codes, plane = w1_ops[a, b]
                    nc.tensor.matmul_mx(
                        out=acc[:],
                        lhsT=codes[:, cols].bitcast(E4M3),
                        lhsT_scale=plane[:, cols],
                        rhs=v_codes[a][:, slits].bitcast(E4M3),
                        rhs_scale=v_scales[4 * a : P, slits],
                        start=(a == 0),
                        stop=(a == PASSES - 1),
                    )
                nc.vector.tensor_tensor(out=page[:, slits], in0=acc[:], in1=page[:, slits], op=ALU.max)

        def pick(picked, scaled, b, t):
            page = pages[b, t]
            nc.vector.tensor_copy(picked[:, t, :], page[:].indirect(error_list[:]))
            column = gain_sb[:, b, t : t + 1]
            if (b, t) == (PASSES - 1, PACK - 1):
                nc.vector.tensor_scalar(
                    out=scaled[:, t, :], in0=picked[:, t, :], scalar1=column, scalar2=None, op0=ALU.mult
                )
            else:
                nc.scalar.activation(out=scaled[:, t, :], in_=picked[:, t, :], func=ACT.Copy, scale=column)

        def scale_page(b, t):
            page = pages[b, t]
            nc.scalar.activation(out=page[:], in_=page[:], func=ACT.Copy, scale=kept_scale[b, t])

        def make_x(picked, azim_rows, x1, x2):
            src = picked[:].rearrange("p t (c i) -> p c t i", i=4)
            nc.scalar.copy(out=x1[:].rearrange("p (c i t) -> p c t i", i=4, t=PACK), in_=src)
            nc.vector.tensor_tensor(
                out=x2[:].rearrange("p (c i t) -> p c t i", i=4, t=PACK),
                in0=src,
                in1=azim_rows[:].rearrange("p t (c i) -> p c t i", i=4),
                op=ALU.mult,
            )

        w3_ops = {}
        picked0 = ring.tile([P, PACK, M], F32, name="picked")
        picked1 = ring.tile([P, PACK, M], F32, name="picked")
        features(0, 0)
        round_weight(raw01, stage[2])
        features(0, 1)
        round_weight(raw11, stage[3])
        pick(picked0, raw11, 0, 0)
        features(0, 2)
        pick(picked0, raw11, 0, 1)
        w1_ops[0, 1] = quantize("w", 4, stage[2])
        make_kept_scale(0)
        features(0, 3)
        pick(picked0, raw11, 0, 2)
        w1_ops[1, 1] = quantize("w", 4, stage[3])
        pick(picked0, raw11, 0, 3)
        features(1, 0)
        make_x(raw11, azim0, stage[0], stage[1])
        features(1, 1)
        round_weight(w3raw00, stage[2])
        round_weight(w3raw10, stage[3])
        round_weight(w3raw01, stage[4])
        pick(picked1, w3raw01, 1, 0)
        x2_ops = [quantize("x2", 2, stage[1])]
        x1_ops = [quantize("x1", 2, stage[0])]
        scale_page(0, 0)
        features(1, 2)
        pick(picked1, w3raw01, 1, 1)
        scale_page(0, 1)
        features(1, 3)
        w3_ops[0, 0] = quantize("w", 4, stage[2])
        pick(picked1, w3raw01, 1, 2)
        pick(picked1, w3raw01, 1, 3)
        w3_ops[1, 0] = quantize("w", 4, stage[3])
        make_x(w3raw01, azim1, stage[0], stage[1])
        x2_ops.append(quantize("x2", 2, stage[1]))
        x1_ops.append(quantize("x1", 2, stage[0]))
        w3_ops[0, 1] = quantize("w", 4, stage[4])
        round_weight(w3raw11, stage[2])
        w3_ops[1, 1] = quantize("w", 4, stage[2])
        make_kept_scale(1)
        make_kept_scale(2)

        first_int = keep.tile([P, M], I32, name="first_int")

        def sine_angle(b, t):
            cols = slice(P * t, P * (t + 1))
            e2 = psum.tile([P, M], F32, name="product_acc", bufs=4)
            for a in range(PASSES):
                codes, plane = w3_ops[a, b]
                nc.tensor.matmul_mx(
                    out=e2[:],
                    lhsT=codes[:, cols].bitcast(E4M3),
                    lhsT_scale=plane[:, cols],
                    rhs=x2_ops[a][0][:].bitcast(E4M3),
                    rhs_scale=x2_ops[a][1][:],
                    start=(a == 0),
                    stop=(a == PASSES - 1),
                )
            turns = ring.tile([P, M], F32, name="turns")
            angle = ring.tile([P, M], F32, name="angle", bufs=3)
            if (b, t) == (0, 0):
                nc.vector.tensor_scalar(
                    out=first_int[:],
                    in0=e2[:],
                    scalar1=1.0 / (2.0 * math.pi),
                    scalar2=ROUND_BIAS,
                    op0=ALU.mult,
                    op1=ALU.add,
                )
                nc.vector.tensor_scalar(
                    out=turns[:], in0=first_int[:], scalar1=-ROUND_BIAS, scalar2=None, op0=ALU.add
                )
            else:
                turns_int = ring.tile([P, M], U32, name="turns_int", bufs=1)
                nc.scalar.activation(
                    out=turns_int[:], in_=e2[:], func=ACT.Copy, scale=1.0 / (2.0 * math.pi), bias=ROUND_BIAS
                )
                nc.scalar.activation(out=turns[:], in_=turns_int[:], func=ACT.Copy, scale=1.0, bias=-ROUND_BIAS)
            nc.vector.scalar_tensor_tensor(
                out=angle[:], in0=turns[:], scalar=-2.0 * math.pi, in1=e2[:], op0=ALU.mult, op1=ALU.add
            )
            return angle

        def tanh_product(b, t):
            n0 = PASS * b + P * t
            e1 = psum.tile([P, M], F32, name="product_acc", bufs=4)
            for a in range(PASSES):
                nc.tensor.matmul_mx(
                    out=e1[:],
                    lhsT=w2_codes[:, a, 2 * n0 : 2 * (n0 + P)].bitcast(E2M1),
                    lhsT_scale=w2_planes[:, a, n0 : n0 + P],
                    rhs=x1_ops[a][0][:].bitcast(E4M3),
                    rhs_scale=x1_ops[a][1][:],
                    start=(a == 0),
                    stop=(a == PASSES - 1),
                )
            tanh_e1 = ring.tile([P, M], F32, name="tanh_e1", bufs=2)
            nc.scalar.activation(out=tanh_e1[:], in_=e1[:], func=ACT.Tanh, bias=zero_bias[:])
            return tanh_e1

        def restore(tanh_e1, angle, b, t):
            page = pages[b, t]
            nc.scalar.activation(out=angle[:], in_=angle[:], func=ACT.Sin, bias=zero_bias[:])
            if b == 0 and t < 1:
                nc.vector.tensor_tensor(out=angle[:], in0=tanh_e1[:], in1=angle[:], op=ALU.add)
                nc.vector.tensor_tensor(out=angle[:], in0=angle[:], in1=wgo_rows[:, t, :], op=ALU.mult)
            else:
                total = ring.tile([P, M], F32, name="total", bufs=1)
                nc.gpsimd.tensor_tensor(out=total[:], in0=tanh_e1[:], in1=angle[:], op=ALU.add)
                nc.gpsimd.tensor_tensor(out=angle[:], in0=total[:], in1=wgo_rows[:, t, :], op=ALU.mult)
            nc.vector.tensor_copy(page[:].indirect(error_list[:]), angle[:])
            nc.sync.dma_start(out=out.rearrange("(b p t) j -> b t p j", p=P, t=PACK)[b, t], in_=page[:])

        order = [(b, t) for b in range(PASSES) for t in range(PACK)]
        angles = [sine_angle(0, 0)]
        for i, (b, t) in enumerate(order):
            tanh_e1 = tanh_product(b, t)
            if i == 0:
                angles.append(sine_angle(*order[1]))
            restore(tanh_e1, angles[i], b, t)
            if i + 2 < len(order):
                angles.append(sine_angle(*order[i + 2]))
            if 1 <= i < len(order) - 1:
                scale_page(*order[i + 1])
